import numpy as np, ml_dtypes
CORES = [1,9,17,25,33,41,49,57,129,257,385]
N = 11
def setup_inputs(rng):
    return {"x": rng.standard_normal((N, 128, 16), dtype=np.float32).astype(ml_dtypes.bfloat16)}
def reference(x):
    s = x.sum(axis=0, dtype=np.float64).astype(x.dtype)
    return {"y": np.broadcast_to(s, (N,) + s.shape)}

@@ -1,0 +1,69 @@
+from concourse.bass import DstId, RemoteDMATransfer
+
+HUBS = {3: [1, 17, 33, 49, 385], 11: [9, 25, 41, 57], 131: [129, 257]}
+HUB_ORDER = [131, 11, 3]
+
+SCRATCH = {
+    "xs": ("dram", [128, 16], "bfloat16"),
+    "inbox": ("dram", [5, 128, 16], "bfloat16"),
+    "part": ("dram", [3, 128, 16], "bfloat16"),
+    "res": ("dram", [128, 16], "bfloat16"),
+}
+SEMAPHORES = ["ld", "a1", "a2", "a3", "st", "snt"]
+
+
+def _bits(m):
+    return bin(m).count("1")
+
+
+def _masks(src, dsts, topo):
+    off = [d for d in dsts if topo.mask(src, d) != 0xFFFF]
+    per = 8
+    while per * len(off) > 8:
+        per //= 2
+    out, k = {}, 0
+    for d in dsts:
+        if d in off:
+            out[d] = ((1 << per) - 1) << (per * k)
+            k += 1
+        else:
+            out[d] = 0xFF00
+    return out
+
+
+def _fold(g, T, topo, core, srcs, dsts, dst_ap, sem):
+    masks = _masks(core, dsts, topo)
+    trs = []
+    for d in dsts:
+        rid, pid = topo.addr(d, core)
+        trs.append(RemoteDMATransfer(dst_ids=[DstId(rid=rid, pnc=pid)], dma_engine_mask=masks[d], remote_sem=sem,
+                                     srcs=srcs, dsts=[dst_ap], alu_op=1))
+    g.remote_dma_fused(trs, local_sem=T.sem.snt)
+    return sum(_bits(m) for m in masks.values())
+
+
+def rank_program(g, core, T, topo):
+    if core in HUBS:
+        ranks = HUBS[core]
+        peers = [h for h in HUB_ORDER if h != core]
+        raw = [T.inbox[i] for i in range(len(ranks))]
+        g.wait_ge(T.sem.a1, sum(_bits(topo.mask(r, core)) for r in ranks))
+        sent = _fold(g, T, topo, core, raw, peers, T.part[HUB_ORDER.index(core)], T.sem.a2)
+        g.wait_ge(T.sem.a2, sum(_bits(_masks(p, [h for h in HUB_ORDER if h != p], topo)[core]) for p in peers))
+        sent += _fold(g, T, topo, core, raw + [T.part[HUB_ORDER.index(p)] for p in peers], ranks, T.res[:, :], T.sem.a3)
+        g.wait_ge(T.sem.snt, sent)
+        return
+
+    if T.rank_of(core) is None:
+        return
+    hub = [h for h in HUBS if core in HUBS[h]][0]
+    g.sync.dma_start(T.xs[:, :], T.x[:, :]).then_inc(T.sem.ld, 16)
+    g.wait_ge(T.sem.ld, 16)
+    rid, pid = topo.addr(hub, core)
+    m = topo.mask(core, hub)
+    g.remote_dma(T.inbox[HUBS[hub].index(core)], T.xs[:, :], remote_sem=T.sem.a1, local_sem=T.sem.snt, pid=pid, routing_id=rid,
+                 dma_engine_mask=m)
+    g.sync.wait_ge(T.sem.a3, _bits(_masks(hub, HUBS[hub], topo)[core]))
+    g.sync.dma_start(T.y[:, :], T.res[:, :]).then_inc(T.sem.st, 16)
+    g.sync.wait_ge(T.sem.st, 16)
+    g.wait_ge(T.sem.snt, _bits(m))

@@ -2,6 +2,7 @@ from concourse.bass import DstId, RemoteDMATransfer
 
 HUBS = {3: [1, 17, 33, 49, 385], 11: [9, 25, 41, 57], 131: [129, 257]}
 HUB_ORDER = [131, 11, 3]
+FOLD_MASK, FOLD_ENGINES = 0x00FF, 8
 
 SCRATCH = {
     "xs": ("dram", [128, 16], "bfloat16"),
@@ -16,30 +17,13 @@ def _bits(m):
     return bin(m).count("1")
 
 
-def _masks(src, dsts, topo):
-    off = [d for d in dsts if topo.mask(src, d) != 0xFFFF]
-    per = 8
-    while per * len(off) > 8:
-        per //= 2
-    out, k = {}, 0
-    for d in dsts:
-        if d in off:
-            out[d] = ((1 << per) - 1) << (per * k)
-            k += 1
-        else:
-            out[d] = 0xFF00
-    return out
-
-
 def _fold(g, T, topo, core, srcs, dsts, dst_ap, sem):
-    masks = _masks(core, dsts, topo)
-    trs = []
+    ids = []
     for d in dsts:
         rid, pid = topo.addr(d, core)
-        trs.append(RemoteDMATransfer(dst_ids=[DstId(rid=rid, pnc=pid)], dma_engine_mask=masks[d], remote_sem=sem,
-                                     srcs=srcs, dsts=[dst_ap], alu_op=1))
-    g.remote_dma_fused(trs, local_sem=T.sem.snt)
-    return sum(_bits(m) for m in masks.values())
+        ids.append(DstId(rid=rid, pnc=pid))
+    g.remote_dma_fused([RemoteDMATransfer(dst_ids=ids, dma_engine_mask=FOLD_MASK, remote_sem=sem, srcs=srcs,
+                                          dsts=[dst_ap for d in dsts], alu_op=1)], local_sem=T.sem.snt)
 
 
 def rank_program(g, core, T, topo):
@@ -48,10 +32,10 @@ def rank_program(g, core, T, topo):
         peers = [h for h in HUB_ORDER if h != core]
         raw = [T.inbox[i] for i in range(len(ranks))]
         g.wait_ge(T.sem.a1, sum(_bits(topo.mask(r, core)) for r in ranks))
-        sent = _fold(g, T, topo, core, raw, peers, T.part[HUB_ORDER.index(core)], T.sem.a2)
-        g.wait_ge(T.sem.a2, sum(_bits(_masks(p, [h for h in HUB_ORDER if h != p], topo)[core]) for p in peers))
-        sent += _fold(g, T, topo, core, raw + [T.part[HUB_ORDER.index(p)] for p in peers], ranks, T.res[:, :], T.sem.a3)
-        g.wait_ge(T.sem.snt, sent)
+        _fold(g, T, topo, core, raw, peers, T.part[HUB_ORDER.index(core)], T.sem.a2)
+        g.wait_ge(T.sem.a2, FOLD_ENGINES * len(peers))
+        _fold(g, T, topo, core, raw + [T.part[HUB_ORDER.index(p)] for p in peers], ranks, T.res[:, :], T.sem.a3)
+        g.wait_ge(T.sem.snt, 2 * FOLD_ENGINES)
         return
 
     if T.rank_of(core) is None:
@@ -63,7 +47,7 @@ def rank_program(g, core, T, topo):
     m = topo.mask(core, hub)
     g.remote_dma(T.inbox[HUBS[hub].index(core)], T.xs[:, :], remote_sem=T.sem.a1, local_sem=T.sem.snt, pid=pid, routing_id=rid,
                  dma_engine_mask=m)
-    g.sync.wait_ge(T.sem.a3, _bits(_masks(hub, HUBS[hub], topo)[core]))
+    g.sync.wait_ge(T.sem.a3, FOLD_ENGINES)
     g.sync.dma_start(T.y[:, :], T.res[:, :]).then_inc(T.sem.st, 16)
     g.sync.wait_ge(T.sem.st, 16)
     g.wait_ge(T.sem.snt, _bits(m))

@@ -1,8 +1,9 @@
 from concourse.bass import DstId, RemoteDMATransfer
 
-HUBS = {3: [1, 17, 33, 49, 385], 11: [9, 25, 41, 57], 131: [129, 257]}
-HUB_ORDER = [131, 11, 3]
-FOLD_MASK, FOLD_ENGINES = 0x00FF, 8
+SETS = [{131: [129, 257, 49], 11: [9, 25, 41, 57], 3: [1, 17, 33, 385]},
+        {403: [385, 257], 27: [9, 25, 41, 57], 19: [1, 17, 33, 49, 129]}]
+SERVE = {3: [1, 33], 19: [17, 49], 11: [9, 41], 27: [25, 57], 131: [129, 257], 403: [385]}
+MASK, ENGINES = 0x00FF, 8
 
 SCRATCH = {
     "xs": ("dram", [128, 16], "bfloat16"),
@@ -13,41 +14,36 @@ SCRATCH = {
 SEMAPHORES = ["ld", "a1", "a2", "a3", "st", "snt"]
 
 
-def _bits(m):
-    return bin(m).count("1")
-
-
-def _fold(g, T, topo, core, srcs, dsts, dst_ap, sem):
+def _send(g, T, topo, core, srcs, dsts, dst_aps, sem):
     ids = []
     for d in dsts:
         rid, pid = topo.addr(d, core)
         ids.append(DstId(rid=rid, pnc=pid))
-    g.remote_dma_fused([RemoteDMATransfer(dst_ids=ids, dma_engine_mask=FOLD_MASK, remote_sem=sem, srcs=srcs,
-                                          dsts=[dst_ap for d in dsts], alu_op=1)], local_sem=T.sem.snt)
+    g.remote_dma_fused([RemoteDMATransfer(dst_ids=ids, dma_engine_mask=MASK, remote_sem=sem, srcs=srcs, dsts=dst_aps,
+                                          alu_op=1 if len(srcs) > 1 else 0)], local_sem=T.sem.snt)
 
 
 def rank_program(g, core, T, topo):
-    if core in HUBS:
-        ranks = HUBS[core]
-        peers = [h for h in HUB_ORDER if h != core]
-        raw = [T.inbox[i] for i in range(len(ranks))]
-        g.wait_ge(T.sem.a1, sum(_bits(topo.mask(r, core)) for r in ranks))
-        _fold(g, T, topo, core, raw, peers, T.part[HUB_ORDER.index(core)], T.sem.a2)
-        g.wait_ge(T.sem.a2, FOLD_ENGINES * len(peers))
-        _fold(g, T, topo, core, raw + [T.part[HUB_ORDER.index(p)] for p in peers], ranks, T.res[:, :], T.sem.a3)
-        g.wait_ge(T.sem.snt, 2 * FOLD_ENGINES)
-        return
+    for hubs in SETS:
+        if core in hubs:
+            order = list(hubs)
+            peers = [h for h in order if h != core]
+            raw = [T.inbox[i] for i in range(len(hubs[core]))]
+            g.wait_ge(T.sem.a1, ENGINES * len(raw))
+            _send(g, T, topo, core, raw, peers, [T.part[order.index(core)] for p in peers], T.sem.a2)
+            g.wait_ge(T.sem.a2, ENGINES * len(peers))
+            _send(g, T, topo, core, raw + [T.part[order.index(p)] for p in peers], SERVE[core],
+                  [T.res[:, :] for r in SERVE[core]], T.sem.a3)
+            g.wait_ge(T.sem.snt, 2 * ENGINES)
+            return
 
     if T.rank_of(core) is None:
         return
-    hub = [h for h in HUBS if core in HUBS[h]][0]
+    mine = [[h for h in hubs if core in hubs[h]][0] for hubs in SETS]
     g.sync.dma_start(T.xs[:, :], T.x[:, :]).then_inc(T.sem.ld, 16)
     g.wait_ge(T.sem.ld, 16)
-    rid, pid = topo.addr(hub, core)
-    m = topo.mask(core, hub)
-    g.remote_dma(T.inbox[HUBS[hub].index(core)], T.xs[:, :], remote_sem=T.sem.a1, local_sem=T.sem.snt, pid=pid, routing_id=rid,
-                 dma_engine_mask=m)
-    g.sync.wait_ge(T.sem.a3, FOLD_ENGINES)
+    _send(g, T, topo, core, [T.xs[:, :]], mine, [T.inbox[SETS[k][h].index(core)] for k, h in enumerate(mine)], T.sem.a1)
+    g.sync.wait_ge(T.sem.a3, ENGINES)
     g.sync.dma_start(T.y[:, :], T.res[:, :]).then_inc(T.sem.st, 16)
     g.sync.wait_ge(T.sem.st, 16)
-    g.wait_ge(T.sem.snt, _bits(m))
+    g.wait_ge(T.sem.snt, ENGINES)

@@ -1,17 +1,21 @@
 from concourse.bass import DstId, RemoteDMATransfer
 
 SETS = [{131: [129, 257, 49], 11: [9, 25, 41, 57], 3: [1, 17, 33, 385]},
-        {403: [385, 257], 27: [9, 25, 41, 57], 19: [1, 17, 33, 49, 129]}]
-SERVE = {3: [1, 33], 19: [17, 49], 11: [9, 41], 27: [25, 57], 131: [129, 257], 403: [385]}
+        {403: [385, 257, 17], 27: [9, 25, 41, 57], 19: [1, 33, 49, 129]}]
+SERVE = {3: [1, 33], 19: [17, 49], 11: [9, 41], 27: [25, 57], 131: [129], 403: [257, 385]}
 MASK, ENGINES = 0x00FF, 8
 
 SCRATCH = {
     "xs": ("dram", [128, 16], "bfloat16"),
-    "inbox": ("dram", [5, 128, 16], "bfloat16"),
+    "inbox": ("dram", [4, 128, 16], "bfloat16"),
     "part": ("dram", [3, 128, 16], "bfloat16"),
     "res": ("dram", [128, 16], "bfloat16"),
 }
 SEMAPHORES = ["ld", "a1", "a2", "a3", "st", "snt"]
+
+
+def _finisher(hub):
+    return hub - 1
 
 
 def _send(g, T, topo, core, srcs, dsts, dst_aps, sem):
@@ -21,20 +25,22 @@ def _send(g, T, topo, core, srcs, dsts, dst_aps, sem):
         ids.append(DstId(rid=rid, pnc=pid))
     g.remote_dma_fused([RemoteDMATransfer(dst_ids=ids, dma_engine_mask=MASK, remote_sem=sem, srcs=srcs, dsts=dst_aps,
                                           alu_op=1 if len(srcs) > 1 else 0)], local_sem=T.sem.snt)
+    g.wait_ge(T.sem.snt, ENGINES)
 
 
 def rank_program(g, core, T, topo):
     for hubs in SETS:
+        order = list(hubs)
         if core in hubs:
-            order = list(hubs)
-            peers = [h for h in order if h != core]
-            raw = [T.inbox[i] for i in range(len(hubs[core]))]
-            g.wait_ge(T.sem.a1, ENGINES * len(raw))
-            _send(g, T, topo, core, raw, peers, [T.part[order.index(core)] for p in peers], T.sem.a2)
-            g.wait_ge(T.sem.a2, ENGINES * len(peers))
-            _send(g, T, topo, core, raw + [T.part[order.index(p)] for p in peers], SERVE[core],
-                  [T.res[:, :] for r in SERVE[core]], T.sem.a3)
-            g.wait_ge(T.sem.snt, 2 * ENGINES)
+            g.wait_ge(T.sem.a1, ENGINES * len(hubs[core]))
+            dsts = [_finisher(h) for h in order if h != core] + [_finisher(core)]
+            _send(g, T, topo, core, [T.inbox[i] for i in range(len(hubs[core]))], dsts,
+                  [T.part[order.index(core)] for d in dsts], T.sem.a2)
+            return
+        if core + 1 in hubs:
+            g.wait_ge(T.sem.a2, ENGINES * len(order))
+            ranks = SERVE[core + 1]
+            _send(g, T, topo, core, [T.part[i] for i in range(len(order))], ranks, [T.res[:, :] for r in ranks], T.sem.a3)
             return
 
     if T.rank_of(core) is None:
@@ -42,8 +48,7 @@ def rank_program(g, core, T, topo):
     mine = [[h for h in hubs if core in hubs[h]][0] for hubs in SETS]
     g.sync.dma_start(T.xs[:, :], T.x[:, :]).then_inc(T.sem.ld, 16)
     g.wait_ge(T.sem.ld, 16)
-    _send(g, T, topo, core, [T.xs[:, :]], mine, [T.inbox[SETS[k][h].index(core)] for k, h in enumerate(mine)], T.sem.a1)
     g.sync.wait_ge(T.sem.a3, ENGINES)
     g.sync.dma_start(T.y[:, :], T.res[:, :]).then_inc(T.sem.st, 16)
     g.sync.wait_ge(T.sem.st, 16)
-    g.wait_ge(T.sem.snt, ENGINES)
+    _send(g, T, topo, core, [T.xs[:, :]], mine, [T.inbox[SETS[k][h].index(core)] for k, h in enumerate(mine)], T.sem.a1)

@@ -2,14 +2,14 @@ from concourse.bass import DstId, RemoteDMATransfer
 
 SETS = [{131: [129, 257, 49], 11: [9, 25, 41, 57], 3: [1, 17, 33, 385]},
         {403: [385, 257, 17], 27: [9, 25, 41, 57], 19: [1, 33, 49, 129]}]
-SERVE = {3: [1, 33], 19: [17, 49], 11: [9, 41], 27: [25, 57], 131: [129], 403: [257, 385]}
-MASK, ENGINES = 0x00FF, 8
+FOLD_MASK, FOLD_ENGINES = 0x00FF, 8
+HALF_MASKS, HALF_ENGINES = [0x000F, 0x00F0], 4
 
 SCRATCH = {
-    "xs": ("dram", [128, 16], "bfloat16"),
-    "inbox": ("dram", [4, 128, 16], "bfloat16"),
-    "part": ("dram", [3, 128, 16], "bfloat16"),
-    "res": ("dram", [128, 16], "bfloat16"),
+    "xs": ("dram", [2, 128, 8], "bfloat16"),
+    "inbox": ("dram", [4, 128, 8], "bfloat16"),
+    "part": ("dram", [3, 128, 8], "bfloat16"),
+    "res": ("dram", [2, 128, 8], "bfloat16"),
 }
 SEMAPHORES = ["ld", "a1", "a2", "a3", "st", "snt"]
 
@@ -18,37 +18,44 @@ def _finisher(hub):
     return hub - 1
 
 
-def _send(g, T, topo, core, srcs, dsts, dst_aps, sem):
-    ids = []
+def _ids(topo, core, dsts):
+    out = []
     for d in dsts:
         rid, pid = topo.addr(d, core)
-        ids.append(DstId(rid=rid, pnc=pid))
-    g.remote_dma_fused([RemoteDMATransfer(dst_ids=ids, dma_engine_mask=MASK, remote_sem=sem, srcs=srcs, dsts=dst_aps,
-                                          alu_op=1 if len(srcs) > 1 else 0)], local_sem=T.sem.snt)
-    g.wait_ge(T.sem.snt, ENGINES)
+        out.append(DstId(rid=rid, pnc=pid))
+    return out
+
+
+def _fold(g, T, topo, core, srcs, dsts, dst_ap, sem):
+    g.remote_dma_fused([RemoteDMATransfer(dst_ids=_ids(topo, core, dsts), dma_engine_mask=FOLD_MASK, remote_sem=sem, srcs=srcs,
+                                          dsts=[dst_ap for d in dsts], alu_op=1)], local_sem=T.sem.snt)
+    g.wait_ge(T.sem.snt, FOLD_ENGINES)
 
 
 def rank_program(g, core, T, topo):
-    for hubs in SETS:
+    for k, hubs in enumerate(SETS):
         order = list(hubs)
         if core in hubs:
-            g.wait_ge(T.sem.a1, ENGINES * len(hubs[core]))
-            dsts = [_finisher(h) for h in order if h != core] + [_finisher(core)]
-            _send(g, T, topo, core, [T.inbox[i] for i in range(len(hubs[core]))], dsts,
-                  [T.part[order.index(core)] for d in dsts], T.sem.a2)
+            g.wait_ge(T.sem.a1, HALF_ENGINES * len(hubs[core]))
+            _fold(g, T, topo, core, [T.inbox[i] for i in range(len(hubs[core]))],
+                  [_finisher(h) for h in order if h != core] + [_finisher(core)], T.part[order.index(core)], T.sem.a2)
             return
         if core + 1 in hubs:
-            g.wait_ge(T.sem.a2, ENGINES * len(order))
-            ranks = SERVE[core + 1]
-            _send(g, T, topo, core, [T.part[i] for i in range(len(order))], ranks, [T.res[:, :] for r in ranks], T.sem.a3)
+            g.wait_ge(T.sem.a2, FOLD_ENGINES * len(order))
+            _fold(g, T, topo, core, [T.part[i] for i in range(len(order))], hubs[core + 1], T.res[k], T.sem.a3)
             return
 
     if T.rank_of(core) is None:
         return
-    mine = [[h for h in hubs if core in hubs[h]][0] for hubs in SETS]
-    g.sync.dma_start(T.xs[:, :], T.x[:, :]).then_inc(T.sem.ld, 16)
-    g.wait_ge(T.sem.ld, 16)
-    g.sync.wait_ge(T.sem.a3, ENGINES)
-    g.sync.dma_start(T.y[:, :], T.res[:, :]).then_inc(T.sem.st, 16)
+    g.sync.dma_start(T.xs[:, :, :], T.x[:, :]).then_inc(T.sem.ld, 16)
+    g.sync.wait_ge(T.sem.a3, 2 * FOLD_ENGINES)
+    g.sync.dma_start(T.y[:, :], T.res[:, :, :]).then_inc(T.sem.st, 16)
     g.sync.wait_ge(T.sem.st, 16)
-    _send(g, T, topo, core, [T.xs[:, :]], mine, [T.inbox[SETS[k][h].index(core)] for k, h in enumerate(mine)], T.sem.a1)
+    g.wait_ge(T.sem.ld, 16)
+    trs = []
+    for k, hubs in enumerate(SETS):
+        hub = [h for h in hubs if core in hubs[h]][0]
+        trs.append(RemoteDMATransfer(dst_ids=_ids(topo, core, [hub]), dma_engine_mask=HALF_MASKS[k], remote_sem=T.sem.a1,
+                                     srcs=[T.xs[k]], dsts=[T.inbox[hubs[hub].index(core)]], alu_op=0))
+    g.remote_dma_fused(trs, local_sem=T.sem.snt)
+    g.wait_ge(T.sem.snt, 2 * HALF_ENGINES)

from concourse.bass import DstId, RemoteDMATransfer

SETS = [{131: [129, 257, 49], 11: [9, 25, 41, 57], 3: [1, 17, 33, 385]},
        {403: [385, 257, 17], 27: [9, 25, 41, 57], 19: [1, 33, 49, 129]}]
FOLD_MASK, FOLD_ENGINES = 0x00FF, 8
HALF_MASKS, HALF_ENGINES = [0x000F, 0x00F0], 4

SCRATCH = {
    "xs": ("dram", [2, 128, 8], "bfloat16"),
    "inbox": ("dram", [4, 128, 8], "bfloat16"),
    "part": ("dram", [3, 128, 8], "bfloat16"),
    "res": ("dram", [2, 128, 8], "bfloat16"),
}
SEMAPHORES = ["ld", "a1", "a2", "a3", "st", "snt"]


def _finisher(hub):
    return hub - 1


def _ids(topo, core, dsts):
    out = []
    for d in dsts:
        rid, pid = topo.addr(d, core)
        out.append(DstId(rid=rid, pnc=pid))
    return out


def _fold(g, T, topo, core, srcs, dsts, dst_ap, sem):
    g.remote_dma_fused([RemoteDMATransfer(dst_ids=_ids(topo, core, dsts), dma_engine_mask=FOLD_MASK, remote_sem=sem, srcs=srcs,
                                          dsts=[dst_ap for d in dsts], alu_op=1)], local_sem=T.sem.snt)
    g.wait_ge(T.sem.snt, FOLD_ENGINES)


def rank_program(g, core, T, topo):
    for k, hubs in enumerate(SETS):
        order = list(hubs)
        if core in hubs:
            g.wait_ge(T.sem.a1, HALF_ENGINES * len(hubs[core]))
            _fold(g, T, topo, core, [T.inbox[i] for i in range(len(hubs[core]))],
                  [_finisher(h) for h in order if h != core] + [_finisher(core)], T.part[order.index(core)], T.sem.a2)
            return
        if core + 1 in hubs:
            g.wait_ge(T.sem.a2, FOLD_ENGINES * len(order))
            _fold(g, T, topo, core, [T.part[i] for i in range(len(order))], hubs[core + 1], T.res[k], T.sem.a3)
            return

    if T.rank_of(core) is None:
        return
    g.sync.dma_start(T.xs[:, :, :], T.x[:, :]).then_inc(T.sem.ld, 16)
    g.sync.wait_ge(T.sem.a3, 2 * FOLD_ENGINES)
    g.sync.dma_start(T.y[:, :], T.res[:, :, :]).then_inc(T.sem.st, 16)
    g.sync.wait_ge(T.sem.st, 16)
    g.wait_ge(T.sem.ld, 16)
    trs = []
    for k, hubs in enumerate(SETS):
        hub = [h for h in hubs if core in hubs[h]][0]
        trs.append(RemoteDMATransfer(dst_ids=_ids(topo, core, [hub]), dma_engine_mask=HALF_MASKS[k], remote_sem=T.sem.a1,
                                     srcs=[T.xs[k]], dsts=[T.inbox[hubs[hub].index(core)]], alu_op=0))
    g.remote_dma_fused(trs, local_sem=T.sem.snt)
    g.wait_ge(T.sem.snt, 2 * HALF_ENGINES)
